import numpy as np
import ml_dtypes


def mxq(x, axis, fmt="e4m3"):
    dtype, down = {"e4m3": (ml_dtypes.float8_e4m3fn, 7), "e5m2": (ml_dtypes.float8_e5m2, 14)}[fmt]
    v = np.moveaxis(np.asarray(x, np.float32).astype(ml_dtypes.bfloat16).astype(np.float64), axis, -1)
    blocks = v.reshape(v.shape[:-1] + (-1, 32))
    amax = np.abs(blocks).max(-1, keepdims=True)
    byte = np.maximum(np.where(amax > 0, np.frexp(amax)[1] - 1 + 127, 0) - down, 1)
    scale = np.exp2(byte - 127.0)
    codes = (blocks / scale).astype(np.float32).astype(dtype).astype(np.float64)
    return np.moveaxis((codes * scale).reshape(v.shape), -1, axis)


WIDE = False


def mx_kscale(k):
    if not WIDE:
        return np.ones(k)
    levels = np.array([10, -10, 5, -5, 0])
    if k % 512:
        return np.exp2(np.random.permutation(np.resize(levels, k // 32))).repeat(32)
    a = np.empty((k // 512, 16))
    for p in range(k // 512):
        a[p, :8] = np.random.permutation(np.resize(levels, 8))
        for g in range(8):
            far = levels[np.abs(levels - a[p, g]) >= 10]
            a[p, g + 8] = far[np.random.randint(len(far))]
    return np.exp2(a.ravel()).repeat(32)


def f64(x):
    return np.asarray(x).astype(np.float64)


def striped(idx):
    return np.tile(np.asarray(idx).reshape(-1, 16).T, (8, 1)).astype(np.uint16)


def unstriped(offs):
    return offs[:16].T.reshape(-1).astype(np.int64)


E2M1 = np.array([0.0, 0.5, 1.0, 1.5, 2.0, 3.0, 4.0, 6.0, -0.0, -0.5, -1.0, -1.5, -2.0, -3.0, -4.0, -6.0])


def pack_weight(w, fmt):
    k, n = w.shape
    w = f64(np.asarray(w, np.float32).astype(ml_dtypes.bfloat16)).reshape(k // 32, 32, n)
    amax = np.abs(w).max(1)
    if fmt == "e4m3":
        byte = np.frexp(amax)[1] - 1 + 127 - 7
    else:
        mant, ex = np.frexp(amax / 6.0)
        byte = np.where(mant > 0.5, ex, ex - 1) + 127
    byte = np.clip(np.where(amax > 0, byte, 1), 1, 254)
    scaled = (w * np.exp2(127.0 - byte)[:, None, :]).reshape(k, n).astype(np.float32)
    by_word = np.ascontiguousarray(scaled.reshape(k // 512, 128, 4, n).transpose(0, 1, 3, 2))
    if fmt == "e4m3":
        words = by_word.astype(ml_dtypes.float8_e4m3fn).view(np.uint8)
    else:
        c = by_word.astype(ml_dtypes.float4_e2m1fn).view(np.uint8) & 0xF
        words = (c[..., 0::2] | (c[..., 1::2] << 4)).reshape(k // 512, 128, 2 * n)
    return np.ascontiguousarray(words), np.ascontiguousarray(byte.astype(np.uint8).reshape(k // 512, 16, n))


def unpack_weight(words, scales, fmt):
    g, _, n = scales.shape
    words = np.ascontiguousarray(words).reshape(g, 128, n, -1)
    if fmt == "e4m3":
        vals = words.view(ml_dtypes.float8_e4m3fn).astype(np.float64)
    else:
        nib = np.empty((g, 128, n, 4), np.uint8)
        nib[..., 0::2] = words & 0xF
        nib[..., 1::2] = words >> 4
        vals = E2M1[nib]
    vals = vals * np.repeat(np.exp2(scales.astype(np.float64) - 127.0), 8, axis=1)[..., None]
    return vals.transpose(0, 1, 3, 2).reshape(g * 512, n)


def sigmoid(v):
    return 1.0 / (1.0 + np.exp(-v))


K, T, I, D, E, Q = 512, 2048, 512, 512, 512, 256


def setup_inputs():
    n = np.random.standard_normal
    idx = np.random.permutation(T)[:I]
    fk = mx_kscale(K)
    fd = mx_kscale(D)
    fi = mx_kscale(I)
    embp = pack_weight(n((K, T)) / fk[:, None], "e4m3")
    return {
        "emb_words": embp[0],
        "emb_scales": embp[1],
        "wk": (n((K, D)) * 1 / np.sqrt(K) * fk[:, None] / fd).astype(np.float32),
        "wv": (n((K, E)) * 1 / np.sqrt(K) * fk[:, None]).astype(np.float32),
        "query": (n((D, Q)) * 2.0 / np.sqrt(D) * fd[:, None]).astype(np.float32),
        "th": (np.random.uniform(0.0, 1.0, (Q, 1))).astype(np.float32),
        "conf": (np.random.uniform(0.05, 0.2, (1, I)) * fi).astype(np.float32),
        "vsc": (np.random.uniform(0.5, 2.0, (I, 1)) / fi[:, None]).astype(np.float32),
        "res": (n((Q, E)) * 1.5).astype(np.float32),
        "offs": striped(idx),
    }


def reference(emb_words, emb_scales, wk, wv, query, th, conf, vsc, res, offs):
    idx = unstriped(offs)
    embu = unpack_weight(emb_words, emb_scales, "e4m3")
    wkq = mxq(f64(wk), 0, "e4m3")
    embidxg = embu[:, idx]
    key = wkq.T @ embidxg
    queryq = mxq(f64(query), 0, "e4m3")
    keyq = mxq(key, 0, "e4m3")
    a = queryq.T @ keyq
    w = sigmoid(a - f64(th)) * f64(conf)
    wt = w.T
    wvq = mxq(f64(wv), 0, "e4m3")
    v = embidxg.T @ wvq
    vv = v * f64(vsc)
    wtq = mxq(wt, 0, "e4m3")
    vvq = mxq(vv, 0, "e4m3")
    b = wtq.T @ vvq
    y = b + f64(res)
    return y

@@ -1,0 +1,179 @@
+from contextlib import ExitStack
+
+import concourse.mybir as mybir
+from concourse.masks import make_identity
+
+K, T, I, D, E, Q = 512, 2048, 512, 512, 512, 256
+FLOPS = 2 * (K * D * I + D * Q * I + K * I * E + I * Q * E)
+
+F32 = mybir.dt.float32
+BF16 = mybir.dt.bfloat16
+I32 = mybir.dt.int32
+U32 = mybir.dt.uint32
+U16 = mybir.dt.uint16
+U8 = mybir.dt.uint8
+FP8X4 = mybir.dt.float8_e4m3fn_x4
+MULT = mybir.AluOpType.mult
+ADD = mybir.AluOpType.add
+SIGMOID = mybir.ActivationFunctionType.Sigmoid
+
+P = 128
+PACK = 4
+BANK = 512
+
+
+def interleave(copy, dst, src):
+    copy(
+        out=dst.rearrange("p (c i) j -> p c j i", i=4),
+        in_=src.rearrange("p j (c i) -> p c j i", i=4),
+    )
+
+
+def quantize(nc, codes, scales, values):
+    nc.vector.quantize_mx(out=codes.bitcast(FP8X4), scales=scales, in_=values)
+
+
+def mx(nc, out, lhs, lhs_s, rhs, rhs_s):
+    nc.tensor.matmul_mx(
+        out=out, lhsT=lhs.bitcast(FP8X4), lhsT_scale=lhs_s, rhs=rhs.bitcast(FP8X4), rhs_scale=rhs_s, start=True, stop=True
+    )
+
+
+def tile_attend_retro_kernel(tc, emb_words, emb_scales, wk, wv, query, th, conf, vsc, res, offs, out):
+    nc = tc.nc
+    with ExitStack() as ctx:
+        held = ctx.enter_context(tc.tile_pool(name="held", bufs=1))
+        sb = ctx.enter_context(tc.tile_pool(name="sb", bufs=1))
+        ps = ctx.enter_context(tc.psum_pool(name="ps", bufs=1))
+
+        offsets = held.tile([P, I // 16], U16, name="offsets")
+        nc.sync.dma_start(offsets[:], offs)
+
+        store_scales = sb.tile([P, T], U8, name="store_scales", align_bytes=64)
+        nc.vector.memset(store_scales[:].bitcast(I32), 0)
+        for g in range(4):
+            nc.scalar.dma_start(
+                store_scales[32 * g : 32 * g + 4, :].bitcast(I32), emb_scales[0, 4 * g : 4 * g + 4, :].bitcast(I32)
+            )
+
+        wk_raw = sb.tile([P, PACK, D], F32, name="wk_raw", tag="wk_then_res")
+        nc.sync.dma_start(wk_raw[:], wk.rearrange("(p j) d -> p j d", j=PACK))
+        store_words = sb.tile([P, T], I32, name="store_words", align_bytes=64)
+        nc.sync.dma_start(store_words[:], emb_words[0].rearrange("p n t -> p (n t)").bitcast(I32))
+        query_raw = sb.tile([P, PACK, Q], F32, name="query_raw")
+        nc.sync.dma_start(query_raw[:], query.rearrange("(p j) q -> p j q", j=PACK))
+        wv_raw = sb.tile([P, PACK, E], F32, name="wv_raw")
+        nc.sync.dma_start(wv_raw[:], wv.rearrange("(p j) e -> p j e", j=PACK))
+
+        th_sb = sb.tile([P, 2], F32, name="th_sb")
+        with nc.allow_non_contiguous_dma(reason="one threshold a partition"):
+            nc.gpsimd.dma_start(th_sb[:], th.rearrange("(c p) o -> p (c o)", p=P))
+        vsc_sb = sb.tile([P, PACK], F32, name="vsc_sb")
+        nc.gpsimd.dma_start(vsc_sb[:], vsc.rearrange("(p t) o -> p (t o)", t=PACK))
+        conf_sb = sb.tile([P, PACK], F32, name="conf_sb")
+        nc.gpsimd.dma_start(conf_sb[:], conf.rearrange("o (p t) -> p (o t)", t=PACK))
+        ident = sb.tile([P, P], F32, name="ident")
+        make_identity(nc, ident[:])
+        neg_th = sb.tile([P, 2], F32, name="neg_th")
+        nc.gpsimd.tensor_scalar(neg_th[:], th_sb[:], -1.0, 0.0, MULT, ADD)
+
+        warm = sb.tile([P, 1], F32, name="warm")
+        nc.scalar.activation(warm[:], ident[:, 0:1], SIGMOID)
+
+        picked_scales = sb.tile([P, I], U8, name="picked_scales", align_bytes=64)
+        nc.vector.tensor_copy(picked_scales[:], store_scales[:].indirect(offsets[:]))
+        emb_s = sb.tile([P, I], U8, name="emb_s", align_bytes=64)
+        nc.vector.tensor_copy(emb_s[:].rearrange("p (t m) -> p m t", t=PACK), picked_scales[:].rearrange("p (m t) -> p m t", t=PACK))
+
+        wk_bf = sb.tile([P, PACK, P, PACK], BF16, name="wk_bf", align_bytes=64)
+        wk_src = wk_raw[:].rearrange("p j (m t) -> p m j t", t=PACK)
+        wk_dst = wk_bf[:].rearrange("p t m j -> p m j t")
+        nc.scalar.copy(out=wk_dst[:, 0:64], in_=wk_src[:, 0:64])
+        nc.vector.tensor_copy(out=wk_dst[:, 64:128], in_=wk_src[:, 64:128])
+        wk_c = sb.tile([P, D], U32, name="wk_c", align_bytes=64)
+        wk_s = sb.tile([P, D], U8, name="wk_s", align_bytes=64)
+        quantize(nc, wk_c[:], wk_s[:], wk_bf[:].rearrange("p t m j -> p (t m j)"))
+
+        res_sb = sb.tile([P, 2, E], F32, name="res_sb", tag="wk_then_res")
+        nc.sync.dma_start(res_sb[:], res.rearrange("(c p) e -> p c e", p=P))
+
+        emb_c = sb.tile([P, I], U32, name="emb_c", align_bytes=64)
+        nc.vector.tensor_copy(emb_c[:].rearrange("p (t m) -> p m t", t=PACK), store_words[:].bitcast(U32).indirect(offsets[:]))
+
+        query_bf = sb.tile([P, Q, PACK], BF16, name="query_bf", align_bytes=64)
+        interleave(nc.scalar.copy, query_bf[:], query_raw[:])
+        query_c = sb.tile([P, Q], U32, name="query_c", align_bytes=64)
+        query_s = sb.tile([P, Q], U8, name="query_s", align_bytes=64)
+
+        key_c = sb.tile([P, I], U32, name="key_c", align_bytes=64)
+        key_s = sb.tile([P, I], U8, name="key_s", align_bytes=64)
+        key_bf = []
+        for b in range(4):
+            cols = slice(b * P, (b + 1) * P)
+            bank = ps.tile([P, PACK, P], F32, name=f"key_bank{b}", tag="chain", bufs=5)
+            for t in range(PACK):
+                dcols = slice(t * P, (t + 1) * P)
+                mx(nc, bank[:, t, :], wk_c[:, dcols], wk_s[:, dcols], emb_c[:, cols], emb_s[:, cols])
+            kb = sb.tile([P, P, PACK], BF16, name=f"key_bf{b}", align_bytes=64)
+            if b % 2 == 0:
+                nc.vector.tensor_copy(kb[:], bank[:].rearrange("p t i -> p i t"))
+            else:
+                nc.scalar.copy(kb[:], bank[:].rearrange("p t i -> p i t"))
+            key_bf.append(kb)
+        quantize(nc, query_c[:], query_s[:], query_bf[:].rearrange("p q j -> p (q j)"))
+        for b in range(4):
+            cols = slice(b * P, (b + 1) * P)
+            quantize(nc, key_c[:, cols], key_s[:, cols], key_bf[b][:].rearrange("p i t -> p (i t)"))
+
+        turned = []
+        for c in range(2):
+            qcols = slice(c * P, (c + 1) * P)
+            scores = ps.tile([P, I], F32, name=f"scores{c}", tag="chain", bufs=5)
+            mx(nc, scores[:], query_c[:, qcols], query_s[:, qcols], key_c[:], key_s[:])
+            gate = sb.tile([P, I], F32, name=f"gate{c}")
+            nc.scalar.activation(gate[:], scores[:], SIGMOID, bias=neg_th[:, c : c + 1])
+            tb = ps.tile([P, PACK, P], F32, name=f"turned{c}", tag="chain", bufs=5)
+            for t in range(PACK):
+                nc.tensor.transpose(tb[:, t, :], gate[:, t * P : (t + 1) * P], ident[:])
+            turned.append(tb)
+
+        wv_c = sb.tile([P, E], U32, name="wv_c", align_bytes=64)
+        wv_s = sb.tile([P, E], U8, name="wv_s", align_bytes=64)
+        vv_c = sb.tile([P, E], U32, name="vv_c", align_bytes=64)
+        vv_s = sb.tile([P, E], U8, name="vv_s", align_bytes=64)
+        vsc_b = vsc_sb[:].unsqueeze(1).to_broadcast([P, P, PACK])
+        vv_bf = []
+        for b in range(4):
+            cols = slice(b * P, (b + 1) * P)
+            wb = sb.tile([P, P, PACK], BF16, name=f"wv_bf{b}", align_bytes=64)
+            interleave(nc.scalar.copy, wb[:], wv_raw[:, :, cols])
+            quantize(nc, wv_c[:, cols], wv_s[:, cols], wb[:].rearrange("p e j -> p (e j)"))
+            bank = ps.tile([P, PACK, P], F32, name=f"v_bank{b}", tag="values", bufs=3)
+            for t in range(PACK):
+                icols = slice(t * P, (t + 1) * P)
+                mx(nc, bank[:, t, :], emb_c[:, icols], emb_s[:, icols], wv_c[:, cols], wv_s[:, cols])
+            vb = sb.tile([P, P, PACK], BF16, name=f"vv_bf{b}", align_bytes=64)
+            nc.vector.tensor_tensor(vb[:], bank[:].rearrange("p t e -> p e t"), vsc_b, MULT)
+            vv_bf.append(vb)
+        for b in range(4):
+            cols = slice(b * P, (b + 1) * P)
+            quantize(nc, vv_c[:, cols], vv_s[:, cols], vv_bf[b][:].rearrange("p e t -> p (e t)"))
+
+        conf_b = conf_sb[:].unsqueeze(1).to_broadcast([P, P, PACK])
+        wt_c = sb.tile([P, Q], U32, name="wt_c", align_bytes=64)
+        wt_s = sb.tile([P, Q], U8, name="wt_s", align_bytes=64)
+        wt_bf = []
+        for c in range(2):
+            wtb = sb.tile([P, P, PACK], BF16, name=f"wt_bf{c}", align_bytes=64)
+            nc.vector.tensor_tensor(wtb[:], turned[c][:].rearrange("p t q -> p q t"), conf_b, MULT)
+            wt_bf.append(wtb)
+        for c in range(2):
+            qcols = slice(c * P, (c + 1) * P)
+            quantize(nc, wt_c[:, qcols], wt_s[:, qcols], wt_bf[c][:].rearrange("p q t -> p (q t)"))
+        for c in range(2):
+            qcols = slice(c * P, (c + 1) * P)
+            mixed = ps.tile([P, E], F32, name=f"mixed{c}", tag="chain", bufs=5)
+            mx(nc, mixed[:], wt_c[:, qcols], wt_s[:, qcols], vv_c[:], vv_s[:])
+            result = sb.tile([P, E], F32, name=f"result{c}")
+            nc.vector.tensor_tensor(result[:], mixed[:], res_sb[:, c, :], ADD)
+            nc.sync.dma_start(out[qcols, :], result[:])

@@ -16,10 +16,18 @@ FP8X4 = mybir.dt.float8_e4m3fn_x4
 MULT = mybir.AluOpType.mult
 ADD = mybir.AluOpType.add
 SIGMOID = mybir.ActivationFunctionType.Sigmoid
+COPY = mybir.ActivationFunctionType.Copy
 
 P = 128
-PACK = 4
-BANK = 512
+PLACES = 4
+RUN = 4
+HALF = 256
+MX_ALIGN = 64
+CHAIN_BANKS, VALUE_BANKS = 5, 3
+
+
+def cols(n, width=P):
+    return slice(n * width, (n + 1) * width)
 
 
 def interleave(copy, dst, src):
@@ -29,151 +37,207 @@ def interleave(copy, dst, src):
     )
 
 
-def quantize(nc, codes, scales, values):
-    nc.vector.quantize_mx(out=codes.bitcast(FP8X4), scales=scales, in_=values)
-
-
-def mx(nc, out, lhs, lhs_s, rhs, rhs_s):
-    nc.tensor.matmul_mx(
-        out=out, lhsT=lhs.bitcast(FP8X4), lhsT_scale=lhs_s, rhs=rhs.bitcast(FP8X4), rhs_scale=rhs_s, start=True, stop=True
-    )
-
-
 def tile_attend_retro_kernel(tc, emb_words, emb_scales, wk, wv, query, th, conf, vsc, res, offs, out):
     nc = tc.nc
+
     with ExitStack() as ctx:
         held = ctx.enter_context(tc.tile_pool(name="held", bufs=1))
         sb = ctx.enter_context(tc.tile_pool(name="sb", bufs=1))
         ps = ctx.enter_context(tc.psum_pool(name="ps", bufs=1))
 
-        offsets = held.tile([P, I // 16], U16, name="offsets")
-        nc.sync.dma_start(offsets[:], offs)
+        def mx_operand(name, width):
+            words = sb.tile([P, width], U32, name=name + "_words", align_bytes=MX_ALIGN)
+            scales = sb.tile([P, width], U8, name=name + "_scales", align_bytes=MX_ALIGN)
+            return words, scales
 
-        store_scales = sb.tile([P, T], U8, name="store_scales", align_bytes=64)
-        nc.vector.memset(store_scales[:].bitcast(I32), 0)
-        for g in range(4):
-            nc.scalar.dma_start(
-                store_scales[32 * g : 32 * g + 4, :].bitcast(I32), emb_scales[0, 4 * g : 4 * g + 4, :].bitcast(I32)
+        def bf16_tile(name, width):
+            return sb.tile([P, width, PLACES], BF16, name=name, align_bytes=MX_ALIGN)
+
+        def quantize(operand, columns, values):
+            words, scales = operand
+            nc.vector.quantize_mx(
+                out=words[:, columns].bitcast(FP8X4),
+                scales=scales[:, columns],
+                in_=values.rearrange("p n t -> p (n t)"),
             )
 
-        wk_raw = sb.tile([P, PACK, D], F32, name="wk_raw", tag="wk_then_res")
-        nc.sync.dma_start(wk_raw[:], wk.rearrange("(p j) d -> p j d", j=PACK))
-        store_words = sb.tile([P, T], I32, name="store_words", align_bytes=64)
-        nc.sync.dma_start(store_words[:], emb_words[0].rearrange("p n t -> p (n t)").bitcast(I32))
-        query_raw = sb.tile([P, PACK, Q], F32, name="query_raw")
-        nc.sync.dma_start(query_raw[:], query.rearrange("(p j) q -> p j q", j=PACK))
-        wv_raw = sb.tile([P, PACK, E], F32, name="wv_raw")
-        nc.sync.dma_start(wv_raw[:], wv.rearrange("(p j) e -> p j e", j=PACK))
+        def mx_pass(dst, stationary, stationary_cols, moving, moving_cols):
+            nc.tensor.matmul_mx(
+                out=dst,
+                lhsT=stationary[0][:, stationary_cols].bitcast(FP8X4),
+                lhsT_scale=stationary[1][:, stationary_cols],
+                rhs=moving[0][:, moving_cols].bitcast(FP8X4),
+                rhs_scale=moving[1][:, moving_cols],
+                start=True,
+                stop=True,
+            )
+
+        store_scales = sb.tile([P, T], U8, name="store_scales", align_bytes=MX_ALIGN)
+        nc.gpsimd.memset(store_scales[:].bitcast(I32), 0)
+        offsets = held.tile([P, I // 16], U16, name="offsets")
+        nc.sync.dma_start(offsets[:], offs)
+        store_words = sb.tile([P, T], I32, name="store_words", tag="store_then_res", align_bytes=MX_ALIGN)
+        words_hbm = emb_words[0].rearrange("p n t -> p (n t)").bitcast(I32)
+        nc.sync.dma_start(store_words[:, cols(0, T // 2)], words_hbm[:, cols(0, T // 2)])
+        for r in range(4):
+            nc.sync.dma_start(store_scales[r:P:32, :].bitcast(I32), emb_scales[0, r:16:4, :].bitcast(I32))
+        nc.sync.dma_start(store_words[:, cols(1, T // 2)], words_hbm[:, cols(1, T // 2)])
+
+        def load_rows(name, matrix, columns, width):
+            raw = sb.tile([P, PLACES, width], F32, name=name)
+            nc.sync.dma_start(raw[:], matrix.rearrange("(p j) n -> p j n", j=PLACES)[:, :, columns])
+            return raw
+
+        wk_raw = [load_rows(f"wk_raw{h}", wk, cols(h, HALF), HALF) for h in range(2)]
+        query_raw = load_rows("query_raw", query, cols(0, Q), Q)
+        wv_raw = [load_rows(f"wv_raw{h}", wv, cols(h, HALF), HALF) for h in range(2)]
 
         th_sb = sb.tile([P, 2], F32, name="th_sb")
-        with nc.allow_non_contiguous_dma(reason="one threshold a partition"):
+        with nc.allow_non_contiguous_dma(reason="one threshold a partition and query half"):
             nc.gpsimd.dma_start(th_sb[:], th.rearrange("(c p) o -> p (c o)", p=P))
-        vsc_sb = sb.tile([P, PACK], F32, name="vsc_sb")
-        nc.gpsimd.dma_start(vsc_sb[:], vsc.rearrange("(p t) o -> p (t o)", t=PACK))
-        conf_sb = sb.tile([P, PACK], F32, name="conf_sb")
-        nc.gpsimd.dma_start(conf_sb[:], conf.rearrange("o (p t) -> p (o t)", t=PACK))
+        group = PLACES * RUN
+        slot_raw = sb.tile([P, 2, PLACES, RUN], F32, name="slot_raw")
+        for a, vector in enumerate((vsc.rearrange("(u x) o -> u o x", x=group), conf.rearrange("o (u x) -> u o x", x=group))):
+            nc.gpsimd.dma_start(slot_raw[:, a].rearrange("p t r -> p (t r)"), vector.to_broadcast([P // RUN, RUN, group]))
+
         ident = sb.tile([P, P], F32, name="ident")
         make_identity(nc, ident[:])
+
+        table_preload = sb.tile([P, 1], F32, name="table_preload")
+        nc.scalar.activation(table_preload[:], th_sb[:, 0:1], SIGMOID)
+
         neg_th = sb.tile([P, 2], F32, name="neg_th")
         nc.gpsimd.tensor_scalar(neg_th[:], th_sb[:], -1.0, 0.0, MULT, ADD)
 
-        warm = sb.tile([P, 1], F32, name="warm")
-        nc.scalar.activation(warm[:], ident[:, 0:1], SIGMOID)
+        lane = ident
+        for width in (64, 32, 16, 8, RUN):
+            folded = sb.tile([P, width], F32, name=f"folded{width}")
+            nc.gpsimd.tensor_tensor(folded[:], lane[:, cols(0, width)], lane[:, cols(1, width)], ADD)
+            lane = folded
+        slot_masked = sb.tile([P, 2 * PLACES, RUN], F32, name="slot_masked")
+        nc.gpsimd.tensor_tensor(
+            slot_masked[:],
+            slot_raw[:].rearrange("p a t r -> p (a t) r"),
+            lane[:].unsqueeze(1).to_broadcast([P, 2 * PLACES, RUN]),
+            MULT,
+        )
+        slot_pair = sb.tile([P, 2 * PLACES, 2], F32, name="slot_pair")
+        nc.gpsimd.tensor_tensor(slot_pair[:], slot_masked[:, :, 0:2], slot_masked[:, :, 2:4], ADD)
+        slot_factor = sb.tile([P, 2 * PLACES], F32, name="slot_factor")
+        nc.gpsimd.tensor_tensor(slot_factor[:], slot_pair[:, :, 0], slot_pair[:, :, 1], ADD)
+        vsc_by_place = slot_factor[:, cols(0, PLACES)].unsqueeze(1).to_broadcast([P, P, PLACES])
+        conf_by_place = slot_factor[:, cols(1, PLACES)].unsqueeze(1).to_broadcast([P, P, PLACES])
 
-        picked_scales = sb.tile([P, I], U8, name="picked_scales", align_bytes=64)
+        picked_scales = sb.tile([P, I], U8, name="picked_scales", align_bytes=MX_ALIGN)
         nc.vector.tensor_copy(picked_scales[:], store_scales[:].indirect(offsets[:]))
-        emb_s = sb.tile([P, I], U8, name="emb_s", align_bytes=64)
-        nc.vector.tensor_copy(emb_s[:].rearrange("p (t m) -> p m t", t=PACK), picked_scales[:].rearrange("p (m t) -> p m t", t=PACK))
+        listed = mx_operand("listed", I)
+        nc.vector.tensor_copy(
+            listed[1][:].bitcast(I32).rearrange("p (t u) -> p t u", t=PLACES),
+            picked_scales[:].bitcast(I32).rearrange("p (u t) -> p t u", t=PLACES),
+        )
+        nc.vector.tensor_copy(
+            listed[0][:].rearrange("p (t u r) -> p u t r", t=PLACES, r=RUN),
+            store_words[:].bitcast(U32).indirect(offsets[:]),
+        )
 
-        wk_bf = sb.tile([P, PACK, P, PACK], BF16, name="wk_bf", align_bytes=64)
-        wk_src = wk_raw[:].rearrange("p j (m t) -> p m j t", t=PACK)
-        wk_dst = wk_bf[:].rearrange("p t m j -> p m j t")
-        nc.scalar.copy(out=wk_dst[:, 0:64], in_=wk_src[:, 0:64])
-        nc.vector.tensor_copy(out=wk_dst[:, 64:128], in_=wk_src[:, 64:128])
-        wk_c = sb.tile([P, D], U32, name="wk_c", align_bytes=64)
-        wk_s = sb.tile([P, D], U8, name="wk_s", align_bytes=64)
-        quantize(nc, wk_c[:], wk_s[:], wk_bf[:].rearrange("p t m j -> p (t m j)"))
-
-        res_sb = sb.tile([P, 2, E], F32, name="res_sb", tag="wk_then_res")
+        res_sb = sb.tile([P, 2, E], F32, name="res_sb", tag="store_then_res", align_bytes=MX_ALIGN)
         nc.sync.dma_start(res_sb[:], res.rearrange("(c p) e -> p c e", p=P))
 
-        emb_c = sb.tile([P, I], U32, name="emb_c", align_bytes=64)
-        nc.vector.tensor_copy(emb_c[:].rearrange("p (t m) -> p m t", t=PACK), store_words[:].bitcast(U32).indirect(offsets[:]))
+        wk_mx = mx_operand("wk", D)
+        wk_bf = [sb.tile([P, 2, P, PLACES], BF16, name=f"wk_bf{a}", align_bytes=MX_ALIGN) for a in range(2)]
+        for h in range(2):
+            src = wk_raw[h][:].rearrange("p j (m t) -> p m j t", t=PLACES)
+            for a, copy in enumerate((nc.scalar.copy, nc.vector.tensor_copy)):
+                dst = wk_bf[a][:].rearrange("p t m j -> p m j t")
+                copy(out=dst[:, cols(h, HALF // PLACES)], in_=src[:, :, :, cols(a, 2)])
+        for a in (1, 0):
+            quantize(wk_mx, cols(a, HALF), wk_bf[a][:].rearrange("p t m j -> p (t m) j"))
 
-        query_bf = sb.tile([P, Q, PACK], BF16, name="query_bf", align_bytes=64)
-        interleave(nc.scalar.copy, query_bf[:], query_raw[:])
-        query_c = sb.tile([P, Q], U32, name="query_c", align_bytes=64)
-        query_s = sb.tile([P, Q], U8, name="query_s", align_bytes=64)
+        key_bank = []
+        for b in range(4):
+            bank = ps.tile([P, PLACES, P], F32, name=f"key_bank{b}", tag="chain", bufs=CHAIN_BANKS)
+            for t in (2, 3, 0, 1):
+                mx_pass(bank[:, t, :], wk_mx, cols(t), listed, cols(b))
+            key_bank.append(bank)
 
-        key_c = sb.tile([P, I], U32, name="key_c", align_bytes=64)
-        key_s = sb.tile([P, I], U8, name="key_s", align_bytes=64)
-        key_bf = []
+        query_bf = bf16_tile("query_bf", Q)
+        query_mx = mx_operand("query", Q)
+        for c, copy in enumerate((nc.scalar.copy, nc.vector.tensor_copy)):
+            interleave(copy, query_bf[:, cols(c), :], query_raw[:, :, cols(c)])
+        quantize(query_mx, cols(0, Q), query_bf[:])
+
+        key_bf = bf16_tile("key_bf", I)
+        key_mx = mx_operand("key", I)
         for b in range(4):
-            cols = slice(b * P, (b + 1) * P)
-            bank = ps.tile([P, PACK, P], F32, name=f"key_bank{b}", tag="chain", bufs=5)
-            for t in range(PACK):
-                dcols = slice(t * P, (t + 1) * P)
-                mx(nc, bank[:, t, :], wk_c[:, dcols], wk_s[:, dcols], emb_c[:, cols], emb_s[:, cols])
-            kb = sb.tile([P, P, PACK], BF16, name=f"key_bf{b}", align_bytes=64)
-            if b % 2 == 0:
-                nc.vector.tensor_copy(kb[:], bank[:].rearrange("p t i -> p i t"))
-            else:
-                nc.scalar.copy(kb[:], bank[:].rearrange("p t i -> p i t"))
-            key_bf.append(kb)
-        quantize(nc, query_c[:], query_s[:], query_bf[:].rearrange("p q j -> p (q j)"))
-        for b in range(4):
-            cols = slice(b * P, (b + 1) * P)
-            quantize(nc, key_c[:, cols], key_s[:, cols], key_bf[b][:].rearrange("p i t -> p (i t)"))
+            nc.scalar.copy(key_bf[:, cols(b), :], key_bank[b][:].rearrange("p t n -> p n t"))
+
+        wv_bf = bf16_tile("wv_bf", E)
+        wv_mx = mx_operand("wv", E)
+        value_bank = []
+
+        def multiply_values(h, copies):
+            for n, copy in enumerate(copies):
+                interleave(copy, wv_bf[:, cols(2 * h + n), :], wv_raw[h][:, :, cols(n)])
+            quantize(wv_mx, cols(h, HALF), wv_bf[:, cols(h, HALF), :])
+            for b in (2 * h, 2 * h + 1):
+                bank = ps.tile([P, PLACES, P], F32, name=f"value_bank{b}", tag="values", bufs=VALUE_BANKS)
+                for t in range(PLACES):
+                    mx_pass(bank[:, t, :], listed, cols(t), wv_mx, cols(b))
+                value_bank.append(bank)
+
+        multiply_values(0, (nc.vector.tensor_copy, nc.vector.tensor_copy))
+        for h in range(2):
+            quantize(key_mx, cols(h, HALF), key_bf[:, cols(h, HALF), :])
+        multiply_values(1, (nc.vector.tensor_copy, nc.scalar.copy))
+
+        score_bank = []
+        for h in range(2):
+            bank = ps.tile([P, 2, HALF], F32, name=f"score_bank{h}", tag="chain", bufs=CHAIN_BANKS)
+            for c in range(2):
+                mx_pass(bank[:, c, :], query_mx, cols(c), key_mx, cols(h, HALF))
+            score_bank.append(bank)
 
         turned = []
         for c in range(2):
-            qcols = slice(c * P, (c + 1) * P)
-            scores = ps.tile([P, I], F32, name=f"scores{c}", tag="chain", bufs=5)
-            mx(nc, scores[:], query_c[:, qcols], query_s[:, qcols], key_c[:], key_s[:])
             gate = sb.tile([P, I], F32, name=f"gate{c}")
-            nc.scalar.activation(gate[:], scores[:], SIGMOID, bias=neg_th[:, c : c + 1])
-            tb = ps.tile([P, PACK, P], F32, name=f"turned{c}", tag="chain", bufs=5)
-            for t in range(PACK):
-                nc.tensor.transpose(tb[:, t, :], gate[:, t * P : (t + 1) * P], ident[:])
-            turned.append(tb)
+            for h in range(2):
+                nc.scalar.activation(gate[:, cols(h, HALF)], score_bank[h][:, c, :], SIGMOID, bias=neg_th[:, cols(c, 1)])
+            bank = ps.tile([P, PLACES, P], F32, name=f"turned{c}", tag="chain", bufs=CHAIN_BANKS)
+            for t in range(PLACES):
+                nc.tensor.transpose(bank[:, t, :], gate[:, cols(t)], ident[:])
+            turned.append(bank)
 
-        wv_c = sb.tile([P, E], U32, name="wv_c", align_bytes=64)
-        wv_s = sb.tile([P, E], U8, name="wv_s", align_bytes=64)
-        vv_c = sb.tile([P, E], U32, name="vv_c", align_bytes=64)
-        vv_s = sb.tile([P, E], U8, name="vv_s", align_bytes=64)
-        vsc_b = vsc_sb[:].unsqueeze(1).to_broadcast([P, P, PACK])
-        vv_bf = []
-        for b in range(4):
-            cols = slice(b * P, (b + 1) * P)
-            wb = sb.tile([P, P, PACK], BF16, name=f"wv_bf{b}", align_bytes=64)
-            interleave(nc.scalar.copy, wb[:], wv_raw[:, :, cols])
-            quantize(nc, wv_c[:, cols], wv_s[:, cols], wb[:].rearrange("p e j -> p (e j)"))
-            bank = ps.tile([P, PACK, P], F32, name=f"v_bank{b}", tag="values", bufs=3)
-            for t in range(PACK):
-                icols = slice(t * P, (t + 1) * P)
-                mx(nc, bank[:, t, :], emb_c[:, icols], emb_s[:, icols], wv_c[:, cols], wv_s[:, cols])
-            vb = sb.tile([P, P, PACK], BF16, name=f"vv_bf{b}", align_bytes=64)
-            nc.vector.tensor_tensor(vb[:], bank[:].rearrange("p t e -> p e t"), vsc_b, MULT)
-            vv_bf.append(vb)
-        for b in range(4):
-            cols = slice(b * P, (b + 1) * P)
-            quantize(nc, vv_c[:, cols], vv_s[:, cols], vv_bf[b][:].rearrange("p e t -> p (e t)"))
+        wt_bf = bf16_tile("wt_bf", Q)
+        wt_mx = mx_operand("wt", Q)
+        for c in range(2):
+            nc.vector.tensor_tensor(wt_bf[:, cols(c), :], turned[c][:].rearrange("p t n -> p n t"), conf_by_place, MULT)
+            quantize(wt_mx, cols(c), wt_bf[:, cols(c), :])
 
-        conf_b = conf_sb[:].unsqueeze(1).to_broadcast([P, P, PACK])
-        wt_c = sb.tile([P, Q], U32, name="wt_c", align_bytes=64)
-        wt_s = sb.tile([P, Q], U8, name="wt_s", align_bytes=64)
-        wt_bf = []
-        for c in range(2):
-            wtb = sb.tile([P, P, PACK], BF16, name=f"wt_bf{c}", align_bytes=64)
-            nc.vector.tensor_tensor(wtb[:], turned[c][:].rearrange("p t q -> p q t"), conf_b, MULT)
-            wt_bf.append(wtb)
-        for c in range(2):
-            qcols = slice(c * P, (c + 1) * P)
-            quantize(nc, wt_c[:, qcols], wt_s[:, qcols], wt_bf[c][:].rearrange("p q t -> p (q t)"))
-        for c in range(2):
-            qcols = slice(c * P, (c + 1) * P)
-            mixed = ps.tile([P, E], F32, name=f"mixed{c}", tag="chain", bufs=5)
-            mx(nc, mixed[:], wt_c[:, qcols], wt_s[:, qcols], vv_c[:], vv_s[:])
-            result = sb.tile([P, E], F32, name=f"result{c}")
-            nc.vector.tensor_tensor(result[:], mixed[:], res_sb[:, c, :], ADD)
-            nc.sync.dma_start(out[qcols, :], result[:])
+        vv_bf = bf16_tile("vv_bf", E)
+        vv_mx = mx_operand("vv", E)
+
+        def scale_values_on_vector(b):
+            nc.vector.tensor_tensor(vv_bf[:, cols(b), :], value_bank[b][:].rearrange("p t n -> p n t"), vsc_by_place, MULT)
+
+        def scale_values_on_scalar(b):
+            planar = sb.tile([P, PLACES, P], BF16, name="vv_planar")
+            for t in range(PLACES):
+                nc.scalar.activation(planar[:, t, :], value_bank[b][:, t, :], COPY, scale=slot_factor[:, cols(t, 1)])
+            nc.scalar.copy(vv_bf[:, cols(b), :], planar[:].rearrange("p t n -> p n t"))
+
+        scale_values_on_vector(0)
+        scale_values_on_vector(1)
+        quantize(vv_mx, cols(0, HALF), vv_bf[:, cols(0, HALF), :])
+        scale_values_on_scalar(2)
+        scale_values_on_vector(3)
+        quantize(vv_mx, cols(1, HALF), vv_bf[:, cols(1, HALF), :])
+
+        quarters = [(c, h) for c in range(2) for h in range(2)]
+        mixed = {}
+        for c, h in quarters:
+            mixed[c, h] = ps.tile([P, HALF], F32, name=f"mixed{c}{h}", tag="chain", bufs=CHAIN_BANKS)
+            mx_pass(mixed[c, h][:], wt_mx, cols(c), vv_mx, cols(h, HALF))
+        for c, h in quarters:
+            result = sb.tile([P, HALF], F32, name=f"result{c}{h}")
+            nc.vector.tensor_tensor(result[:], mixed[c, h][:], res_sb[:, c, cols(h, HALF)], ADD)
+            nc.sync.dma_start(out[cols(c), cols(h, HALF)], result[:])

from contextlib import ExitStack

import concourse.mybir as mybir
from concourse.masks import make_identity

K, T, I, D, E, Q = 512, 2048, 512, 512, 512, 256
FLOPS = 2 * (K * D * I + D * Q * I + K * I * E + I * Q * E)

F32 = mybir.dt.float32
BF16 = mybir.dt.bfloat16
I32 = mybir.dt.int32
U32 = mybir.dt.uint32
U16 = mybir.dt.uint16
U8 = mybir.dt.uint8
FP8X4 = mybir.dt.float8_e4m3fn_x4
MULT = mybir.AluOpType.mult
ADD = mybir.AluOpType.add
SIGMOID = mybir.ActivationFunctionType.Sigmoid
COPY = mybir.ActivationFunctionType.Copy

P = 128
PLACES = 4
RUN = 4
HALF = 256
MX_ALIGN = 64
CHAIN_BANKS, VALUE_BANKS = 5, 3


def cols(n, width=P):
    return slice(n * width, (n + 1) * width)


def interleave(copy, dst, src):
    copy(
        out=dst.rearrange("p (c i) j -> p c j i", i=4),
        in_=src.rearrange("p j (c i) -> p c j i", i=4),
    )


def tile_attend_retro_kernel(tc, emb_words, emb_scales, wk, wv, query, th, conf, vsc, res, offs, out):
    nc = tc.nc

    with ExitStack() as ctx:
        held = ctx.enter_context(tc.tile_pool(name="held", bufs=1))
        sb = ctx.enter_context(tc.tile_pool(name="sb", bufs=1))
        ps = ctx.enter_context(tc.psum_pool(name="ps", bufs=1))

        def mx_operand(name, width):
            words = sb.tile([P, width], U32, name=name + "_words", align_bytes=MX_ALIGN)
            scales = sb.tile([P, width], U8, name=name + "_scales", align_bytes=MX_ALIGN)
            return words, scales

        def bf16_tile(name, width):
            return sb.tile([P, width, PLACES], BF16, name=name, align_bytes=MX_ALIGN)

        def quantize(operand, columns, values):
            words, scales = operand
            nc.vector.quantize_mx(
                out=words[:, columns].bitcast(FP8X4),
                scales=scales[:, columns],
                in_=values.rearrange("p n t -> p (n t)"),
            )

        def mx_pass(dst, stationary, stationary_cols, moving, moving_cols):
            nc.tensor.matmul_mx(
                out=dst,
                lhsT=stationary[0][:, stationary_cols].bitcast(FP8X4),
                lhsT_scale=stationary[1][:, stationary_cols],
                rhs=moving[0][:, moving_cols].bitcast(FP8X4),
                rhs_scale=moving[1][:, moving_cols],
                start=True,
                stop=True,
            )

        store_scales = sb.tile([P, T], U8, name="store_scales", align_bytes=MX_ALIGN)
        nc.gpsimd.memset(store_scales[:].bitcast(I32), 0)
        offsets = held.tile([P, I // 16], U16, name="offsets")
        nc.sync.dma_start(offsets[:], offs)
        store_words = sb.tile([P, T], I32, name="store_words", tag="store_then_res", align_bytes=MX_ALIGN)
        words_hbm = emb_words[0].rearrange("p n t -> p (n t)").bitcast(I32)
        nc.sync.dma_start(store_words[:, cols(0, T // 2)], words_hbm[:, cols(0, T // 2)])
        for r in range(4):
            nc.sync.dma_start(store_scales[r:P:32, :].bitcast(I32), emb_scales[0, r:16:4, :].bitcast(I32))
        nc.sync.dma_start(store_words[:, cols(1, T // 2)], words_hbm[:, cols(1, T // 2)])

        def load_rows(name, matrix, columns, width):
            raw = sb.tile([P, PLACES, width], F32, name=name)
            nc.sync.dma_start(raw[:], matrix.rearrange("(p j) n -> p j n", j=PLACES)[:, :, columns])
            return raw

        wk_raw = [load_rows(f"wk_raw{h}", wk, cols(h, HALF), HALF) for h in range(2)]
        query_raw = load_rows("query_raw", query, cols(0, Q), Q)
        wv_raw = [load_rows(f"wv_raw{h}", wv, cols(h, HALF), HALF) for h in range(2)]

        th_sb = sb.tile([P, 2], F32, name="th_sb")
        with nc.allow_non_contiguous_dma(reason="one threshold a partition and query half"):
            nc.gpsimd.dma_start(th_sb[:], th.rearrange("(c p) o -> p (c o)", p=P))
        group = PLACES * RUN
        slot_raw = sb.tile([P, 2, PLACES, RUN], F32, name="slot_raw")
        for a, vector in enumerate((vsc.rearrange("(u x) o -> u o x", x=group), conf.rearrange("o (u x) -> u o x", x=group))):
            nc.gpsimd.dma_start(slot_raw[:, a].rearrange("p t r -> p (t r)"), vector.to_broadcast([P // RUN, RUN, group]))

        ident = sb.tile([P, P], F32, name="ident")
        make_identity(nc, ident[:])

        table_preload = sb.tile([P, 1], F32, name="table_preload")
        nc.scalar.activation(table_preload[:], th_sb[:, 0:1], SIGMOID)

        neg_th = sb.tile([P, 2], F32, name="neg_th")
        nc.gpsimd.tensor_scalar(neg_th[:], th_sb[:], -1.0, 0.0, MULT, ADD)

        lane = ident
        for width in (64, 32, 16, 8, RUN):
            folded = sb.tile([P, width], F32, name=f"folded{width}")
            nc.gpsimd.tensor_tensor(folded[:], lane[:, cols(0, width)], lane[:, cols(1, width)], ADD)
            lane = folded
        slot_masked = sb.tile([P, 2 * PLACES, RUN], F32, name="slot_masked")
        nc.gpsimd.tensor_tensor(
            slot_masked[:],
            slot_raw[:].rearrange("p a t r -> p (a t) r"),
            lane[:].unsqueeze(1).to_broadcast([P, 2 * PLACES, RUN]),
            MULT,
        )
        slot_pair = sb.tile([P, 2 * PLACES, 2], F32, name="slot_pair")
        nc.gpsimd.tensor_tensor(slot_pair[:], slot_masked[:, :, 0:2], slot_masked[:, :, 2:4], ADD)
        slot_factor = sb.tile([P, 2 * PLACES], F32, name="slot_factor")
        nc.gpsimd.tensor_tensor(slot_factor[:], slot_pair[:, :, 0], slot_pair[:, :, 1], ADD)
        vsc_by_place = slot_factor[:, cols(0, PLACES)].unsqueeze(1).to_broadcast([P, P, PLACES])
        conf_by_place = slot_factor[:, cols(1, PLACES)].unsqueeze(1).to_broadcast([P, P, PLACES])

        picked_scales = sb.tile([P, I], U8, name="picked_scales", align_bytes=MX_ALIGN)
        nc.vector.tensor_copy(picked_scales[:], store_scales[:].indirect(offsets[:]))
        listed = mx_operand("listed", I)
        nc.vector.tensor_copy(
            listed[1][:].bitcast(I32).rearrange("p (t u) -> p t u", t=PLACES),
            picked_scales[:].bitcast(I32).rearrange("p (u t) -> p t u", t=PLACES),
        )
        nc.vector.tensor_copy(
            listed[0][:].rearrange("p (t u r) -> p u t r", t=PLACES, r=RUN),
            store_words[:].bitcast(U32).indirect(offsets[:]),
        )

        res_sb = sb.tile([P, 2, E], F32, name="res_sb", tag="store_then_res", align_bytes=MX_ALIGN)
        nc.sync.dma_start(res_sb[:], res.rearrange("(c p) e -> p c e", p=P))

        wk_mx = mx_operand("wk", D)
        wk_bf = [sb.tile([P, 2, P, PLACES], BF16, name=f"wk_bf{a}", align_bytes=MX_ALIGN) for a in range(2)]
        for h in range(2):
            src = wk_raw[h][:].rearrange("p j (m t) -> p m j t", t=PLACES)
            for a, copy in enumerate((nc.scalar.copy, nc.vector.tensor_copy)):
                dst = wk_bf[a][:].rearrange("p t m j -> p m j t")
                copy(out=dst[:, cols(h, HALF // PLACES)], in_=src[:, :, :, cols(a, 2)])
        for a in (1, 0):
            quantize(wk_mx, cols(a, HALF), wk_bf[a][:].rearrange("p t m j -> p (t m) j"))

        key_bank = []
        for b in range(4):
            bank = ps.tile([P, PLACES, P], F32, name=f"key_bank{b}", tag="chain", bufs=CHAIN_BANKS)
            for t in (2, 3, 0, 1):
                mx_pass(bank[:, t, :], wk_mx, cols(t), listed, cols(b))
            key_bank.append(bank)

        query_bf = bf16_tile("query_bf", Q)
        query_mx = mx_operand("query", Q)
        for c, copy in enumerate((nc.scalar.copy, nc.vector.tensor_copy)):
            interleave(copy, query_bf[:, cols(c), :], query_raw[:, :, cols(c)])
        quantize(query_mx, cols(0, Q), query_bf[:])

        key_bf = bf16_tile("key_bf", I)
        key_mx = mx_operand("key", I)
        for b in range(4):
            nc.scalar.copy(key_bf[:, cols(b), :], key_bank[b][:].rearrange("p t n -> p n t"))

        wv_bf = bf16_tile("wv_bf", E)
        wv_mx = mx_operand("wv", E)
        value_bank = []

        def multiply_values(h, copies):
            for n, copy in enumerate(copies):
                interleave(copy, wv_bf[:, cols(2 * h + n), :], wv_raw[h][:, :, cols(n)])
            quantize(wv_mx, cols(h, HALF), wv_bf[:, cols(h, HALF), :])
            for b in (2 * h, 2 * h + 1):
                bank = ps.tile([P, PLACES, P], F32, name=f"value_bank{b}", tag="values", bufs=VALUE_BANKS)
                for t in range(PLACES):
                    mx_pass(bank[:, t, :], listed, cols(t), wv_mx, cols(b))
                value_bank.append(bank)

        multiply_values(0, (nc.vector.tensor_copy, nc.vector.tensor_copy))
        for h in range(2):
            quantize(key_mx, cols(h, HALF), key_bf[:, cols(h, HALF), :])
        multiply_values(1, (nc.vector.tensor_copy, nc.scalar.copy))

        score_bank = []
        for h in range(2):
            bank = ps.tile([P, 2, HALF], F32, name=f"score_bank{h}", tag="chain", bufs=CHAIN_BANKS)
            for c in range(2):
                mx_pass(bank[:, c, :], query_mx, cols(c), key_mx, cols(h, HALF))
            score_bank.append(bank)

        turned = []
        for c in range(2):
            gate = sb.tile([P, I], F32, name=f"gate{c}")
            for h in range(2):
                nc.scalar.activation(gate[:, cols(h, HALF)], score_bank[h][:, c, :], SIGMOID, bias=neg_th[:, cols(c, 1)])
            bank = ps.tile([P, PLACES, P], F32, name=f"turned{c}", tag="chain", bufs=CHAIN_BANKS)
            for t in range(PLACES):
                nc.tensor.transpose(bank[:, t, :], gate[:, cols(t)], ident[:])
            turned.append(bank)

        wt_bf = bf16_tile("wt_bf", Q)
        wt_mx = mx_operand("wt", Q)
        for c in range(2):
            nc.vector.tensor_tensor(wt_bf[:, cols(c), :], turned[c][:].rearrange("p t n -> p n t"), conf_by_place, MULT)
            quantize(wt_mx, cols(c), wt_bf[:, cols(c), :])

        vv_bf = bf16_tile("vv_bf", E)
        vv_mx = mx_operand("vv", E)

        def scale_values_on_vector(b):
            nc.vector.tensor_tensor(vv_bf[:, cols(b), :], value_bank[b][:].rearrange("p t n -> p n t"), vsc_by_place, MULT)

        def scale_values_on_scalar(b):
            planar = sb.tile([P, PLACES, P], BF16, name="vv_planar")
            for t in range(PLACES):
                nc.scalar.activation(planar[:, t, :], value_bank[b][:, t, :], COPY, scale=slot_factor[:, cols(t, 1)])
            nc.scalar.copy(vv_bf[:, cols(b), :], planar[:].rearrange("p t n -> p n t"))

        scale_values_on_vector(0)
        scale_values_on_vector(1)
        quantize(vv_mx, cols(0, HALF), vv_bf[:, cols(0, HALF), :])
        scale_values_on_scalar(2)
        scale_values_on_vector(3)
        quantize(vv_mx, cols(1, HALF), vv_bf[:, cols(1, HALF), :])

        quarters = [(c, h) for c in range(2) for h in range(2)]
        mixed = {}
        for c, h in quarters:
            mixed[c, h] = ps.tile([P, HALF], F32, name=f"mixed{c}{h}", tag="chain", bufs=CHAIN_BANKS)
            mx_pass(mixed[c, h][:], wt_mx, cols(c), vv_mx, cols(h, HALF))
        for c, h in quarters:
            result = sb.tile([P, HALF], F32, name=f"result{c}{h}")
            nc.vector.tensor_tensor(result[:], mixed[c, h][:], res_sb[:, c, cols(h, HALF)], ADD)
            nc.sync.dma_start(out[cols(c), cols(h, HALF)], result[:])
